import numpy as np
import ml_dtypes


def mxq(x, axis, fmt="e4m3"):
    dtype, down = {"e4m3": (ml_dtypes.float8_e4m3fn, 7), "e5m2": (ml_dtypes.float8_e5m2, 14)}[fmt]
    v = np.moveaxis(np.asarray(x, np.float32).astype(ml_dtypes.bfloat16).astype(np.float64), axis, -1)
    blocks = v.reshape(v.shape[:-1] + (-1, 32))
    amax = np.abs(blocks).max(-1, keepdims=True)
    byte = np.maximum(np.where(amax > 0, np.frexp(amax)[1] - 1 + 127, 0) - down, 1)
    scale = np.exp2(byte - 127.0)
    codes = (blocks / scale).astype(np.float32).astype(dtype).astype(np.float64)
    return np.moveaxis((codes * scale).reshape(v.shape), -1, axis)


WIDE = False


def mx_kscale(k):
    if not WIDE:
        return np.ones(k)
    levels = np.array([30, -30])
    if k % 512:
        return np.exp2(np.random.permutation(np.resize(levels, k // 32))).repeat(32)
    a = np.empty((k // 512, 16))
    for p in range(k // 512):
        a[p, :8] = np.random.permutation(np.resize(levels, 8))
        for g in range(8):
            far = levels[np.abs(levels - a[p, g]) >= 10]
            a[p, g + 8] = far[np.random.randint(len(far))]
    return np.exp2(a.ravel()).repeat(32)


def f64(x):
    return np.asarray(x).astype(np.float64)


def striped(idx):
    return np.tile(np.asarray(idx).reshape(-1, 16).T, (8, 1)).astype(np.uint16)


def unstriped(offs):
    return offs[:16].T.reshape(-1).astype(np.int64)


E2M1 = np.array([0.0, 0.5, 1.0, 1.5, 2.0, 3.0, 4.0, 6.0, -0.0, -0.5, -1.0, -1.5, -2.0, -3.0, -4.0, -6.0])


def pack_weight(w, fmt):
    k, n = w.shape
    w = f64(np.asarray(w, np.float32).astype(ml_dtypes.bfloat16)).reshape(k // 32, 32, n)
    amax = np.abs(w).max(1)
    if fmt in ("e4m3", "e5m2"):
        byte = np.frexp(amax)[1] - 1 + 127 - (7 if fmt == "e4m3" else 14)
    else:
        mant, ex = np.frexp(amax / 6.0)
        byte = np.where(mant > 0.5, ex, ex - 1) + 127
    byte = np.clip(np.where(amax > 0, byte, 1), 1, 254)
    scaled = (w * np.exp2(127.0 - byte)[:, None, :]).reshape(k, n).astype(np.float32)
    by_word = np.ascontiguousarray(scaled.reshape(k // 512, 128, 4, n).transpose(0, 1, 3, 2))
    if fmt in ("e4m3", "e5m2"):
        words = by_word.astype(ml_dtypes.float8_e4m3fn if fmt == "e4m3" else ml_dtypes.float8_e5m2).view(np.uint8)
    else:
        c = by_word.astype(ml_dtypes.float4_e2m1fn).view(np.uint8) & 0xF
        words = (c[..., 0::2] | (c[..., 1::2] << 4)).reshape(k // 512, 128, 2 * n)
    return np.ascontiguousarray(words), np.ascontiguousarray(byte.astype(np.uint8).reshape(k // 512, 16, n))


def unpack_weight(words, scales, fmt):
    g, _, n = scales.shape
    words = np.ascontiguousarray(words).reshape(g, 128, n, -1)
    if fmt in ("e4m3", "e5m2"):
        vals = words.view(ml_dtypes.float8_e4m3fn if fmt == "e4m3" else ml_dtypes.float8_e5m2).astype(np.float64)
    else:
        nib = np.empty((g, 128, n, 4), np.uint8)
        nib[..., 0::2] = words & 0xF
        nib[..., 1::2] = words >> 4
        vals = E2M1[nib]
    vals = vals * np.repeat(np.exp2(scales.astype(np.float64) - 127.0), 8, axis=1)[..., None]
    return vals.transpose(0, 1, 3, 2).reshape(g * 512, n)


def bf(x):
    return np.asarray(x, np.float32).astype(ml_dtypes.bfloat16)


def planes(Y):
    r, m = Y.shape
    b = f64(bf(Y)).reshape(r // 32, 32, m)
    amax = np.abs(b).max(1)
    byte = np.clip(np.where(amax > 0, np.frexp(amax)[1] - 1 + 127 - 7, 1), 1, 254)
    codes = (b * np.exp2(127.0 - byte)[:, None, :]).reshape(r, m).astype(np.float32).astype(ml_dtypes.float8_e4m3fn).view(np.uint8)
    words = codes.reshape(r // 512, 128, 4, m).transpose(0, 1, 3, 2)
    return np.ascontiguousarray(words), np.ascontiguousarray(byte.astype(np.uint8).reshape(r // 512, 16, m))


K, T, J, S, R, V, N = 1024, 1024, 256, 512, 512, 512, 512


def setup_inputs():
    n = np.random.standard_normal
    idx = np.random.permutation(T)[:J]
    idx2 = np.random.permutation(S)[:J]
    idx3 = np.random.permutation(V)[:J]
    fk = mx_kscale(K)
    fr = mx_kscale(R)
    wp = pack_weight(n((K, R)) * 1 / np.sqrt(K) * fk[:, None] * fr, "e5m2")
    wbp = pack_weight(n((R, N)) * 1 / np.sqrt(R) / fr[:, None], "e2m1")
    return {
        "xa": (n((K, T))).astype(np.float32),
        "xb": (n((K, S))).astype(np.float32),
        "hb": (np.random.uniform(0.2, 0.9, (K, 1))).astype(np.float32),
        "fk": (np.random.uniform(0.5, 2.0, (K, 1)) / fk[:, None]).astype(np.float32),
        "w_words": wp[0],
        "w_scales": wp[1],
        "tb": (n((R, V)) * 0.7 * fr[:, None]).astype(np.float32),
        "wb_words": wbp[0],
        "wb_scales": wbp[1],
        "hi": (np.random.uniform(0.4, 1.2, (N, 1))).astype(np.float32),
        "rw": (np.random.uniform(0.5, 2.0, (1, J))).astype(np.float32),
        "offs": striped(idx),
        "offs2": striped(idx2),
        "offs3": striped(idx3),
    }


def reference(xa, xb, hb, fk, w_words, w_scales, tb, wb_words, wb_scales, hi, rw, offs, offs2, offs3):
    idx = unstriped(offs)
    idx2 = unstriped(offs2)
    idx3 = unstriped(offs3)
    wu = unpack_weight(w_words, w_scales, "e5m2")
    wbu = unpack_weight(wb_words, wb_scales, "e2m1")
    u = (f64(xa)[:, idx] - np.minimum(f64(xb)[:, idx2], f64(hb))) * f64(fk)
    uq = mxq(u, 0, "e5m2")
    a = wu.T @ uq
    hid = np.maximum(a, f64(tb)[:, idx3])
    hidq = mxq(hid, 0, "e5m2")
    p = wbu.T @ hidq
    y = np.minimum(p - f64(hi), 0.0) * f64(rw)
    words, scales = planes(y)
    return y, words, scales

@@ -1,0 +1,289 @@
+from contextlib import ExitStack
+
+import concourse.mybir as mybir
+from concourse.masks import make_identity
+
+K, T, J, S, R, V, N = 1024, 1024, 256, 512, 512, 512, 512
+FLOPS = 2 * K * R * J + 2 * R * N * J
+
+F32 = mybir.dt.float32
+BF16 = mybir.dt.bfloat16
+I32 = mybir.dt.int32
+U32 = mybir.dt.uint32
+U16 = mybir.dt.uint16
+U8 = mybir.dt.uint8
+E5M2X4 = mybir.dt.float8_e5m2_x4
+E4M3X4 = mybir.dt.float8_e4m3fn_x4
+E2M1X4 = mybir.dt.float4_e2m1fn_x4
+ALU = mybir.AluOpType
+ACT = mybir.ActivationFunctionType
+
+P = 128
+PACK = 4
+PASSES = K // (P * PACK)
+HALF = J // 2
+LIST_COLS = J // 16
+
+
+def tile_list_boundedgaps_abovetable_capped_pl_kernel(
+    tc, xa, xb, hb, fk, w_words, w_scales, tb, wb_words, wb_scales, hi, rw, offs, offs2, offs3, out_0, out_1, out_2
+):
+    nc = tc.nc
+    with ExitStack() as ctx:
+        keep = ctx.enter_context(tc.tile_pool(name="keep", bufs=1))
+        ring = ctx.enter_context(tc.tile_pool(name="ring", bufs=3))
+        psum = ctx.enter_context(tc.psum_pool(name="psum", bufs=1))
+        psum_p = ctx.enter_context(tc.psum_pool(name="psum_p", bufs=6))
+
+        def half_cols(h):
+            return slice(h * HALF, (h + 1) * HALF)
+
+        def half_list(list_tile, h):
+            return list_tile[:, h * LIST_COLS // 2 : (h + 1) * LIST_COLS // 2]
+
+        def woven(values):
+            return values.rearrange("p (c i) t -> p c t i", i=4)
+
+        def by_plane(values):
+            return values.rearrange("p t (c i) -> p c t i", i=4)
+
+        w_sc_raw = keep.tile([P, PASSES * R], U8, name="w_sc_raw")
+        wb_sc_raw = keep.tile([P, N], U8, name="wb_sc_raw")
+        ident = keep.tile([P, P], F32, name="ident")
+        nc.gpsimd.memset(w_sc_raw[:].bitcast(I32), 0)
+        make_identity(nc, ident[:])
+        nc.gpsimd.memset(wb_sc_raw[:].bitcast(I32), 0)
+
+        def load_scale_rows(queue, tile, scales, q):
+            queue.dma_start(
+                out=tile[32 * q : 32 * q + 4, :].bitcast(I32).rearrange("r (a c) -> r a c", a=scales.shape[0]),
+                in_=scales[:, 4 * q : 4 * q + 4, :].bitcast(I32).rearrange("a r c -> r a c"),
+            )
+
+        def load_per_k(queue, name, src, passes):
+            tile = keep.tile([P, passes * PACK], F32, name=name)
+            queue.dma_start(
+                out=tile[:].rearrange("p (a t) -> p a t", t=PACK),
+                in_=src.rearrange("(a p t) o -> p a (t o)", p=P, t=PACK),
+            )
+            return tile
+
+        rw_col = keep.tile([P, 2], F32, name="rw_col")
+        nc.scalar.dma_start(out=rw_col[:], in_=rw.rearrange("o (p e) -> p (o e)", e=2))
+        hi_sb = load_per_k(nc.gpsimd, "hi_sb", hi, 1)
+        for q in range(4):
+            load_scale_rows(nc.gpsimd, wb_sc_raw, wb_scales, q)
+        neg_hi = keep.tile([P, PACK], F32, name="neg_hi")
+        nc.gpsimd.tensor_scalar(out=neg_hi[:], in0=hi_sb[:], scalar1=-1.0, scalar2=None, op0=ALU.mult)
+        wb_sc = keep.tile([P, N], U8, name="wb_sc", align_bytes=64)
+        nc.gpsimd.tensor_copy(
+            out=wb_sc[:].rearrange("p (t m) -> p t m", t=PACK), in_=wb_sc_raw[:].rearrange("p (m t) -> p t m", t=PACK)
+        )
+
+        xa_rows = xa.rearrange("(a p t) c -> a p t c", p=P, t=PACK)
+        xb_rows = xb.rearrange("(a p t) c -> a p t c", p=P, t=PACK)
+        tb_rows = tb.rearrange("(p t) c -> p t c", t=PACK)
+
+        def load_list(name, src):
+            tile = keep.tile([P, LIST_COLS], U16, name=name)
+            nc.sync.dma_start(tile[:], src)
+            return tile
+
+        def load_rows(name, rows, t0, count):
+            tile = keep.tile([P, count, rows.shape[2]], F32, name=name)
+            nc.sync.dma_start(out=tile[:], in_=rows[:, t0 : t0 + count, :])
+            return [tile[:, i, :] for i in range(count)]
+
+        def load_words(name, src):
+            tile = keep.tile([P, src.shape[1]], I32, name=name)
+            nc.sync.dma_start(out=tile[:], in_=src)
+            return tile
+
+        def load_w(a):
+            return load_words(f"w_raw{a}", w_words[a].rearrange("p c t -> p (c t)").bitcast(I32))
+
+        list_b = load_list("list_b", offs2)
+        xb_planes = load_rows("xb_0", xb_rows[0], 0, 4)
+        for q in range(4):
+            load_scale_rows(nc.sync, w_sc_raw, w_scales, q)
+        xb_planes = xb_planes + load_rows("xb_1", xb_rows[1], 0, 4)
+        fk_sb = load_per_k(nc.sync, "fk_sb", fk, PASSES)
+        wb_raw = load_words("wb_raw", wb_words[0].bitcast(I32))
+        list_a = load_list("list_a", offs)
+        hb_sb = load_per_k(nc.sync, "hb_sb", hb, PASSES)
+        xa_planes = load_rows("xa_01", xa_rows[0], 0, 2)
+        xa_planes = xa_planes + load_rows("xa_23", xa_rows[0], 2, 2)
+        xa_planes = xa_planes + load_rows("xa_4", xa_rows[1], 0, 1)
+        xa_planes = xa_planes + load_rows("xa_5", xa_rows[1], 1, 1)
+        list_t = load_list("list_t", offs3)
+        xa_planes = xa_planes + load_rows("xa_6", xa_rows[1], 2, 1)
+        w_raw = [load_w(0)]
+        xa_planes = xa_planes + load_rows("xa_7", xa_rows[1], 3, 1)
+        w_raw = w_raw + [load_w(1)]
+        tb_planes = [load_rows(f"tb_{t}", tb_rows, t, 1)[0] for t in range(PACK)]
+
+        gb = [keep.tile([P, J], F32, name=f"gb{i}") for i in range(PASSES * PACK)]
+        u_bf = [keep.tile([P, J, PACK], BF16, name=f"u_bf{a}", align_bytes=64) for a in range(PASSES)]
+        u_codes = [keep.tile([P, J], U32, name=f"u_codes{a}", align_bytes=64) for a in range(PASSES)]
+        u_scales = [keep.tile([P, J], U8, name=f"u_scales{a}", align_bytes=64) for a in range(PASSES)]
+
+        def gather_b(i):
+            if i % PACK < 2:
+                nc.vector.tensor_copy(gb[i][:], xb_planes[i].indirect(list_b[:]))
+            else:
+                nc.scalar.activation(gb[i][:], xb_planes[i].indirect(list_b[:]), ACT.Copy)
+
+        def gap(i, ga, neg_gap, cols):
+            nc.vector.scalar_tensor_tensor(
+                out=neg_gap[:, cols], in0=gb[i][:, cols], scalar=hb_sb[:, i : i + 1], in1=ga[:, cols],
+                op0=ALU.min, op1=ALU.subtract,
+            )
+
+        def scale_u(i, neg_gap, cols):
+            nc.vector.tensor_scalar(
+                out=u_bf[i // PACK][:, cols, i % PACK], in0=neg_gap[:, cols], scalar1=fk_sb[:, i : i + 1],
+                scalar2=-1.0, op0=ALU.mult, op1=ALU.mult,
+            )
+
+        def quantize(codes, scales, values, cols, x4):
+            nc.vector.quantize_mx(
+                out=codes[:, cols].bitcast(x4), scales=scales[:, cols],
+                in_=values[:, cols, :].rearrange("p j t -> p (j t)"),
+            )
+
+        def whole_plane(i):
+            ga = ring.tile([P, J], F32, name="ga")
+            neg_gap = ring.tile([P, J], F32, name="neg_gap")
+            nc.scalar.activation(ga[:], xa_planes[i].indirect(list_a[:]), ACT.Copy)
+            gap(i, ga, neg_gap, slice(0, J))
+            scale_u(i, neg_gap, slice(0, J))
+
+        def deal(out, in_, groups):
+            nc.vector.tensor_copy(
+                out=out.rearrange("p (g t m) -> p g m t", g=groups, t=PACK),
+                in_=in_.rearrange("p (g m t) -> p g m t", g=groups, t=PACK),
+            )
+
+        rw_ps = psum_p.tile([P, 2, P], F32, name="rw_ps", tag="p_ps")
+        for e in range(2):
+            nc.tensor.transpose(rw_ps[:, e, :], rw_col[:, e : e + 1].to_broadcast([P, P]), ident[:])
+        rw_row = keep.tile([P, J], F32, name="rw_row")
+        nc.scalar.copy(out=rw_row[:].rearrange("p (n e) -> p n e", e=2), in_=rw_ps[:].rearrange("p e n -> p n e"))
+
+        for i in range(PASSES * PACK):
+            gather_b(i)
+
+        wb_dealt = keep.tile([P, N], U16, name="wb_dealt", align_bytes=64)
+        deal(wb_dealt[:], wb_raw[:].bitcast(U16), 1)
+        w_sc = keep.tile([P, PASSES * R], U8, name="w_sc", align_bytes=64)
+        nc.gpsimd.tensor_copy(
+            out=w_sc[:].rearrange("p (a t m) -> p a t m", a=PASSES, t=PACK),
+            in_=w_sc_raw[:].rearrange("p (a m t) -> p a t m", a=PASSES, t=PACK),
+        )
+        neg_fk = keep.tile([P, PACK], F32, name="neg_fk")
+        nc.gpsimd.tensor_scalar(out=neg_fk[:], in0=fk_sb[:, 0:PACK], scalar1=-1.0, scalar2=None, op0=ALU.mult)
+        neg_gaps = keep.tile([P, PACK, J], F32, name="neg_gaps")
+        for i in range(PACK):
+            ga = ring.tile([P, J], F32, name="ga")
+            nc.scalar.activation(ga[:], xa_planes[i].indirect(list_a[:]), ACT.Copy)
+            gap(i, ga, neg_gaps[:, i, :], slice(0, J))
+        nc.vector.tensor_tensor(
+            out=woven(u_bf[0][:]), in0=by_plane(neg_gaps[:]),
+            in1=neg_fk[:].unsqueeze(1).unsqueeze(3).to_broadcast([P, J // 4, PACK, 4]), op=ALU.mult,
+        )
+        quantize(u_codes[0], u_scales[0], u_bf[0], slice(0, J), E5M2X4)
+        whole_plane(4)
+        whole_plane(5)
+        w_dealt = [keep.tile([P, R], I32, name=f"w_dealt{a}", align_bytes=64) for a in range(PASSES)]
+        deal(w_dealt[0][:], w_raw[0][:], 1)
+        whole_plane(6)
+
+        last = PASSES * PACK - 1
+        ga = ring.tile([P, J], F32, name="ga")
+        neg_gap = ring.tile([P, J], F32, name="neg_gap")
+        nc.scalar.activation(ga[:, half_cols(0)], xa_planes[last].indirect(half_list(list_a, 0)), ACT.Copy)
+        nc.vector.tensor_copy(ga[:, half_cols(1)], xa_planes[last].indirect(half_list(list_a, 1)))
+        for h in range(2):
+            gap(last, ga, neg_gap, half_cols(h))
+        deal(w_dealt[1][:], w_raw[1][:], 1)
+        for h in range(2):
+            scale_u(last, neg_gap, half_cols(h))
+        for h in range(2):
+            quantize(u_codes[1], u_scales[1], u_bf[1], half_cols(h), E5M2X4)
+
+        a_ps = [psum.tile([P, PACK, HALF], F32, name=f"a_ps{h}", tag=f"a_ps{h}") for h in range(2)]
+        for a in range(PASSES):
+            for h in range(2):
+                for t in range(PACK):
+                    nc.tensor.matmul_mx(
+                        out=a_ps[h][:, t, :],
+                        lhsT=w_dealt[a][:, t * P : (t + 1) * P].bitcast(E5M2X4),
+                        lhsT_scale=w_sc[:, a * R + t * P : a * R + (t + 1) * P],
+                        rhs=u_codes[a][:, half_cols(h)].bitcast(E5M2X4),
+                        rhs_scale=u_scales[a][:, half_cols(h)],
+                        start=(a == 0 and t == 0),
+                        stop=(a == PASSES - 1 and t == PACK - 1),
+                    )
+
+        gt = keep.tile([P, PACK, J], F32, name="gt")
+        for t in range(2):
+            nc.scalar.activation(gt[:, t, :], tb_planes[t].indirect(list_t[:]), ACT.Copy)
+        nc.vector.tensor_copy(gt[:, 2, :], tb_planes[2].indirect(list_t[:]))
+        nc.scalar.activation(gt[:, PACK - 1, half_cols(0)], tb_planes[PACK - 1].indirect(half_list(list_t, 0)), ACT.Copy)
+        nc.vector.tensor_copy(gt[:, PACK - 1, half_cols(1)], tb_planes[PACK - 1].indirect(half_list(list_t, 1)))
+
+        hid_bf = keep.tile([P, J, PACK], BF16, name="hid_bf", align_bytes=64)
+        hid_codes = keep.tile([P, J], U32, name="hid_codes", align_bytes=64)
+        hid_scales = keep.tile([P, J], U8, name="hid_scales", align_bytes=64)
+        for h in range(2):
+            nc.vector.tensor_tensor(
+                out=woven(hid_bf[:, half_cols(h), :]), in0=by_plane(a_ps[h][:]),
+                in1=by_plane(gt[:, :, half_cols(h)]), op=ALU.max,
+            )
+            quantize(hid_codes, hid_scales, hid_bf, half_cols(h), E5M2X4)
+
+        y_rows = out_0.rearrange("(p t) j -> p t j", t=PACK)
+        y_bf = keep.tile([P, J, PACK], BF16, name="y_bf", align_bytes=64)
+        y_codes = keep.tile([P, J], U32, name="y_codes", align_bytes=64)
+        y_scales = keep.tile([P, J], U8, name="y_scales", align_bytes=64)
+        words_out = out_1[0].rearrange("p j t -> p (j t)").bitcast(I32)
+        below = [keep.tile([P, PACK, HALF], F32, name=f"below{h}") for h in range(2)]
+        y = [keep.tile([P, PACK, HALF], F32, name=f"y{h}") for h in range(2)]
+        for h in range(2):
+            for t in range(PACK):
+                if h == 1 and t >= 2:
+                    p_ps = psum.tile([P, HALF], F32, name="p_ps", tag=f"a_ps{t - 2}")
+                else:
+                    p_ps = psum_p.tile([P, HALF], F32, name="p_ps", tag="p_ps")
+                nc.tensor.matmul_mx(
+                    out=p_ps[:],
+                    lhsT=wb_dealt[:, t * P : (t + 1) * P].bitcast(E2M1X4),
+                    lhsT_scale=wb_sc[:, t * P : (t + 1) * P],
+                    rhs=hid_codes[:, half_cols(h)].bitcast(E5M2X4),
+                    rhs_scale=hid_scales[:, half_cols(h)],
+                    start=True,
+                    stop=True,
+                )
+                if h == 0 and t % 2 == 1:
+                    nc.vector.tensor_scalar(
+                        out=below[h][:, t, :], in0=p_ps[:], scalar1=hi_sb[:, t : t + 1], scalar2=None, op0=ALU.subtract
+                    )
+                else:
+                    nc.scalar.activation(below[h][:, t, :], p_ps[:], ACT.Identity, bias=neg_hi[:, t : t + 1])
+        for h in range(2):
+            nc.vector.scalar_tensor_tensor(
+                out=y[h][:], in0=below[h][:], scalar=0.0,
+                in1=rw_row[:, half_cols(h)].unsqueeze(1).to_broadcast([P, PACK, HALF]),
+                op0=ALU.min, op1=ALU.mult,
+            )
+            nc.sync.dma_start(out=y_rows[:, :, half_cols(h)], in_=y[h][:])
+        nc.scalar.copy(out=woven(y_bf[:, half_cols(0), :]), in_=by_plane(y[0][:]))
+        nc.vector.tensor_copy(out=woven(y_bf[:, half_cols(1), :]), in_=by_plane(y[1][:]))
+        for h in range(2):
+            quantize(y_codes, y_scales, y_bf, half_cols(h), E4M3X4)
+            nc.sync.dma_start(out=words_out[:, half_cols(h)], in_=y_codes[:, half_cols(h)].bitcast(I32))
+        for q in range(4):
+            queue = nc.scalar if q < 2 else nc.sync
+            queue.dma_start(
+                out=out_2[0, 4 * q : 4 * q + 4, :].bitcast(I32), in_=y_scales[32 * q : 32 * q + 4, :].bitcast(I32)
+            )

@@ -41,18 +41,12 @@ def tile_list_boundedgaps_abovetable_capped_pl_kernel(
         def half_list(list_tile, h):
             return list_tile[:, h * LIST_COLS // 2 : (h + 1) * LIST_COLS // 2]
 
-        def woven(values):
-            return values.rearrange("p (c i) t -> p c t i", i=4)
-
-        def by_plane(values):
-            return values.rearrange("p t (c i) -> p c t i", i=4)
-
         w_sc_raw = keep.tile([P, PASSES * R], U8, name="w_sc_raw")
         wb_sc_raw = keep.tile([P, N], U8, name="wb_sc_raw")
         ident = keep.tile([P, P], F32, name="ident")
         nc.gpsimd.memset(w_sc_raw[:].bitcast(I32), 0)
-        make_identity(nc, ident[:])
         nc.gpsimd.memset(wb_sc_raw[:].bitcast(I32), 0)
+        make_identity(nc, ident[:])
 
         def load_scale_rows(queue, tile, scales, q):
             queue.dma_start(
@@ -70,15 +64,6 @@ def tile_list_boundedgaps_abovetable_capped_pl_kernel(
 
         rw_col = keep.tile([P, 2], F32, name="rw_col")
         nc.scalar.dma_start(out=rw_col[:], in_=rw.rearrange("o (p e) -> p (o e)", e=2))
-        hi_sb = load_per_k(nc.gpsimd, "hi_sb", hi, 1)
-        for q in range(4):
-            load_scale_rows(nc.gpsimd, wb_sc_raw, wb_scales, q)
-        neg_hi = keep.tile([P, PACK], F32, name="neg_hi")
-        nc.gpsimd.tensor_scalar(out=neg_hi[:], in0=hi_sb[:], scalar1=-1.0, scalar2=None, op0=ALU.mult)
-        wb_sc = keep.tile([P, N], U8, name="wb_sc", align_bytes=64)
-        nc.gpsimd.tensor_copy(
-            out=wb_sc[:].rearrange("p (t m) -> p t m", t=PACK), in_=wb_sc_raw[:].rearrange("p (m t) -> p t m", t=PACK)
-        )
 
         xa_rows = xa.rearrange("(a p t) c -> a p t c", p=P, t=PACK)
         xb_rows = xb.rearrange("(a p t) c -> a p t c", p=P, t=PACK)
@@ -107,12 +92,16 @@ def tile_list_boundedgaps_abovetable_capped_pl_kernel(
         for q in range(4):
             load_scale_rows(nc.sync, w_sc_raw, w_scales, q)
         xb_planes = xb_planes + load_rows("xb_1", xb_rows[1], 0, 4)
-        fk_sb = load_per_k(nc.sync, "fk_sb", fk, PASSES)
+        for q in range(4):
+            load_scale_rows(nc.sync, wb_sc_raw, wb_scales, q)
         wb_raw = load_words("wb_raw", wb_words[0].bitcast(I32))
+        xa_planes = load_rows("xa_01", xa_rows[0], 0, 2)
         list_a = load_list("list_a", offs)
         hb_sb = load_per_k(nc.sync, "hb_sb", hb, PASSES)
-        xa_planes = load_rows("xa_01", xa_rows[0], 0, 2)
-        xa_planes = xa_planes + load_rows("xa_23", xa_rows[0], 2, 2)
+        fk_sb = load_per_k(nc.sync, "fk_sb", fk, PASSES)
+        xa_planes = xa_planes + load_rows("xa_2", xa_rows[0], 2, 1)
+        xa_planes = xa_planes + load_rows("xa_3", xa_rows[0], 3, 1)
+        hi_sb = load_per_k(nc.sync, "hi_sb", hi, 1)
         xa_planes = xa_planes + load_rows("xa_4", xa_rows[1], 0, 1)
         xa_planes = xa_planes + load_rows("xa_5", xa_rows[1], 1, 1)
         list_t = load_list("list_t", offs3)
@@ -173,24 +162,16 @@ def tile_list_boundedgaps_abovetable_capped_pl_kernel(
         for i in range(PASSES * PACK):
             gather_b(i)
 
+        w_sc = keep.tile([P, PASSES * R], U8, name="w_sc", align_bytes=64)
+        deal(w_sc[:], w_sc_raw[:], PASSES)
+        wb_sc = keep.tile([P, N], U8, name="wb_sc", align_bytes=64)
+        deal(wb_sc[:], wb_sc_raw[:], 1)
         wb_dealt = keep.tile([P, N], U16, name="wb_dealt", align_bytes=64)
         deal(wb_dealt[:], wb_raw[:].bitcast(U16), 1)
-        w_sc = keep.tile([P, PASSES * R], U8, name="w_sc", align_bytes=64)
-        nc.gpsimd.tensor_copy(
-            out=w_sc[:].rearrange("p (a t m) -> p a t m", a=PASSES, t=PACK),
-            in_=w_sc_raw[:].rearrange("p (a m t) -> p a t m", a=PASSES, t=PACK),
-        )
-        neg_fk = keep.tile([P, PACK], F32, name="neg_fk")
-        nc.gpsimd.tensor_scalar(out=neg_fk[:], in0=fk_sb[:, 0:PACK], scalar1=-1.0, scalar2=None, op0=ALU.mult)
-        neg_gaps = keep.tile([P, PACK, J], F32, name="neg_gaps")
         for i in range(PACK):
-            ga = ring.tile([P, J], F32, name="ga")
-            nc.scalar.activation(ga[:], xa_planes[i].indirect(list_a[:]), ACT.Copy)
-            gap(i, ga, neg_gaps[:, i, :], slice(0, J))
-        nc.vector.tensor_tensor(
-            out=woven(u_bf[0][:]), in0=by_plane(neg_gaps[:]),
-            in1=neg_fk[:].unsqueeze(1).unsqueeze(3).to_broadcast([P, J // 4, PACK, 4]), op=ALU.mult,
-        )
+            whole_plane(i)
+        neg_hi = keep.tile([P, PACK], F32, name="neg_hi")
+        nc.scalar.activation(neg_hi[:], hi_sb[:], ACT.Copy, scale=-1.0)
         quantize(u_codes[0], u_scales[0], u_bf[0], slice(0, J), E5M2X4)
         whole_plane(4)
         whole_plane(5)
@@ -228,9 +209,15 @@ def tile_list_boundedgaps_abovetable_capped_pl_kernel(
         gt = keep.tile([P, PACK, J], F32, name="gt")
         for t in range(2):
             nc.scalar.activation(gt[:, t, :], tb_planes[t].indirect(list_t[:]), ACT.Copy)
-        nc.vector.tensor_copy(gt[:, 2, :], tb_planes[2].indirect(list_t[:]))
-        nc.scalar.activation(gt[:, PACK - 1, half_cols(0)], tb_planes[PACK - 1].indirect(half_list(list_t, 0)), ACT.Copy)
-        nc.vector.tensor_copy(gt[:, PACK - 1, half_cols(1)], tb_planes[PACK - 1].indirect(half_list(list_t, 1)))
+        for t, h in ((2, 0), (3, 0), (2, 1)):
+            nc.scalar.activation(gt[:, t, half_cols(h)], tb_planes[t].indirect(half_list(list_t, h)), ACT.Copy)
+        nc.vector.tensor_copy(gt[:, 3, half_cols(1)], tb_planes[3].indirect(half_list(list_t, 1)))
+
+        def woven(values):
+            return values.rearrange("p (c i) t -> p c t i", i=4)
+
+        def by_plane(values):
+            return values.rearrange("p t (c i) -> p c t i", i=4)
 
         hid_bf = keep.tile([P, J, PACK], BF16, name="hid_bf", align_bytes=64)
         hid_codes = keep.tile([P, J], U32, name="hid_codes", align_bytes=64)
@@ -264,21 +251,28 @@ def tile_list_boundedgaps_abovetable_capped_pl_kernel(
                     start=True,
                     stop=True,
                 )
-                if h == 0 and t % 2 == 1:
+                if h == 0 and t % 2 == 0:
                     nc.vector.tensor_scalar(
                         out=below[h][:, t, :], in0=p_ps[:], scalar1=hi_sb[:, t : t + 1], scalar2=None, op0=ALU.subtract
                     )
                 else:
                     nc.scalar.activation(below[h][:, t, :], p_ps[:], ACT.Identity, bias=neg_hi[:, t : t + 1])
-        for h in range(2):
+        def weigh(h, c0, c1):
             nc.vector.scalar_tensor_tensor(
-                out=y[h][:], in0=below[h][:], scalar=0.0,
-                in1=rw_row[:, half_cols(h)].unsqueeze(1).to_broadcast([P, PACK, HALF]),
+                out=y[h][:, :, c0:c1], in0=below[h][:, :, c0:c1], scalar=0.0,
+                in1=rw_row[:, h * HALF + c0 : h * HALF + c1].unsqueeze(1).to_broadcast([P, PACK, c1 - c0]),
                 op0=ALU.min, op1=ALU.mult,
             )
-            nc.sync.dma_start(out=y_rows[:, :, half_cols(h)], in_=y[h][:])
+
+        quarter = HALF // 2
+        weigh(0, 0, HALF)
+        nc.sync.dma_start(out=y_rows[:, :, half_cols(0)], in_=y[0][:])
         nc.scalar.copy(out=woven(y_bf[:, half_cols(0), :]), in_=by_plane(y[0][:]))
-        nc.vector.tensor_copy(out=woven(y_bf[:, half_cols(1), :]), in_=by_plane(y[1][:]))
+        weigh(1, 0, quarter)
+        weigh(1, quarter, HALF)
+        nc.sync.dma_start(out=y_rows[:, :, half_cols(1)], in_=y[1][:])
+        nc.vector.tensor_copy(out=woven(y_bf[:, HALF : HALF + quarter, :]), in_=by_plane(y[1][:, :, 0:quarter]))
+        nc.vector.tensor_copy(out=woven(y_bf[:, HALF + quarter : J, :]), in_=by_plane(y[1][:, :, quarter:HALF]))
         for h in range(2):
             quantize(y_codes, y_scales, y_bf, half_cols(h), E4M3X4)
             nc.sync.dma_start(out=words_out[:, half_cols(h)], in_=y_codes[:, half_cols(h)].bitcast(I32))

@@ -23,6 +23,8 @@ PACK = 4
 PASSES = K // (P * PACK)
 HALF = J // 2
 LIST_COLS = J // 16
+ROW_HB, ROW_FK, VEC_ROWS = 0, 2, 4
+ROW_HI, ROW_RW, LATE_ROWS = 0, 1, 2
 
 
 def tile_list_boundedgaps_abovetable_capped_pl_kernel(
@@ -46,7 +48,6 @@ def tile_list_boundedgaps_abovetable_capped_pl_kernel(
         ident = keep.tile([P, P], F32, name="ident")
         nc.gpsimd.memset(w_sc_raw[:].bitcast(I32), 0)
         nc.gpsimd.memset(wb_sc_raw[:].bitcast(I32), 0)
-        make_identity(nc, ident[:])
 
         def load_scale_rows(queue, tile, scales, q):
             queue.dma_start(
@@ -54,16 +55,17 @@ def tile_list_boundedgaps_abovetable_capped_pl_kernel(
                 in_=scales[:, 4 * q : 4 * q + 4, :].bitcast(I32).rearrange("a r c -> r a c"),
             )
 
-        def load_per_k(queue, name, src, passes):
-            tile = keep.tile([P, passes * PACK], F32, name=name)
-            queue.dma_start(
-                out=tile[:].rearrange("p (a t) -> p a t", t=PACK),
-                in_=src.rearrange("(a p t) o -> p a (t o)", p=P, t=PACK),
-            )
-            return tile
+        for q in range(4):
+            load_scale_rows(nc.gpsimd, wb_sc_raw, wb_scales, q)
+        make_identity(nc, ident[:])
 
-        rw_col = keep.tile([P, 2], F32, name="rw_col")
-        nc.scalar.dma_start(out=rw_col[:], in_=rw.rearrange("o (p e) -> p (o e)", e=2))
+        vec_rows = keep.tile([P, P * PACK], F32, name="vec_rows")
+        nc.vector.memset(vec_rows[:], 0.0)
+        late_rows = keep.tile([P, P * PACK], F32, name="late_rows")
+        nc.vector.memset(late_rows[:], 0.0)
+
+        def load_vec(tile, row, src):
+            nc.sync.dma_start(out=tile[row : row + src.shape[0], 0 : src.shape[1]], in_=src)
 
         xa_rows = xa.rearrange("(a p t) c -> a p t c", p=P, t=PACK)
         xb_rows = xb.rearrange("(a p t) c -> a p t c", p=P, t=PACK)
@@ -92,16 +94,13 @@ def tile_list_boundedgaps_abovetable_capped_pl_kernel(
         for q in range(4):
             load_scale_rows(nc.sync, w_sc_raw, w_scales, q)
         xb_planes = xb_planes + load_rows("xb_1", xb_rows[1], 0, 4)
-        for q in range(4):
-            load_scale_rows(nc.sync, wb_sc_raw, wb_scales, q)
+        load_vec(vec_rows, ROW_HB, hb.rearrange("(a c) o -> a (c o)", a=PASSES))
+        load_vec(vec_rows, ROW_FK, fk.rearrange("(a c) o -> a (c o)", a=PASSES))
         wb_raw = load_words("wb_raw", wb_words[0].bitcast(I32))
-        xa_planes = load_rows("xa_01", xa_rows[0], 0, 2)
         list_a = load_list("list_a", offs)
-        hb_sb = load_per_k(nc.sync, "hb_sb", hb, PASSES)
-        fk_sb = load_per_k(nc.sync, "fk_sb", fk, PASSES)
-        xa_planes = xa_planes + load_rows("xa_2", xa_rows[0], 2, 1)
-        xa_planes = xa_planes + load_rows("xa_3", xa_rows[0], 3, 1)
-        hi_sb = load_per_k(nc.sync, "hi_sb", hi, 1)
+        xa_planes = [load_rows(f"xa_{t}", xa_rows[0], t, 1)[0] for t in range(PACK)]
+        load_vec(late_rows, ROW_RW, rw)
+        load_vec(late_rows, ROW_HI, hi.rearrange("(a c) o -> a (c o)", a=1))
         xa_planes = xa_planes + load_rows("xa_4", xa_rows[1], 0, 1)
         xa_planes = xa_planes + load_rows("xa_5", xa_rows[1], 1, 1)
         list_t = load_list("list_t", offs3)
@@ -110,6 +109,11 @@ def tile_list_boundedgaps_abovetable_capped_pl_kernel(
         xa_planes = xa_planes + load_rows("xa_7", xa_rows[1], 3, 1)
         w_raw = w_raw + [load_w(1)]
         tb_planes = [load_rows(f"tb_{t}", tb_rows, t, 1)[0] for t in range(PACK)]
+
+        vec_cols = keep.tile([P, PACK, VEC_ROWS], F32, name="vec_cols")
+
+        def vec_col(row, t):
+            return vec_cols[:, t, row : row + 1]
 
         gb = [keep.tile([P, J], F32, name=f"gb{i}") for i in range(PASSES * PACK)]
         u_bf = [keep.tile([P, J, PACK], BF16, name=f"u_bf{a}", align_bytes=64) for a in range(PASSES)]
@@ -124,13 +128,13 @@ def tile_list_boundedgaps_abovetable_capped_pl_kernel(
 
         def gap(i, ga, neg_gap, cols):
             nc.vector.scalar_tensor_tensor(
-                out=neg_gap[:, cols], in0=gb[i][:, cols], scalar=hb_sb[:, i : i + 1], in1=ga[:, cols],
+                out=neg_gap[:, cols], in0=gb[i][:, cols], scalar=vec_col(ROW_HB + i // PACK, i % PACK), in1=ga[:, cols],
                 op0=ALU.min, op1=ALU.subtract,
             )
 
         def scale_u(i, neg_gap, cols):
             nc.vector.tensor_scalar(
-                out=u_bf[i // PACK][:, cols, i % PACK], in0=neg_gap[:, cols], scalar1=fk_sb[:, i : i + 1],
+                out=u_bf[i // PACK][:, cols, i % PACK], in0=neg_gap[:, cols], scalar1=vec_col(ROW_FK + i // PACK, i % PACK),
                 scalar2=-1.0, op0=ALU.mult, op1=ALU.mult,
             )
 
@@ -147,32 +151,52 @@ def tile_list_boundedgaps_abovetable_capped_pl_kernel(
             gap(i, ga, neg_gap, slice(0, J))
             scale_u(i, neg_gap, slice(0, J))
 
+        def deal_narrow(out, in_, groups):
+            nc.vector.tensor_copy(
+                out=out.rearrange("p (g t m) -> p g t m", g=groups, t=PACK),
+                in_=in_.rearrange("p (g m t) -> p g t m", g=groups, t=PACK),
+            )
+
         def deal(out, in_, groups):
             nc.vector.tensor_copy(
                 out=out.rearrange("p (g t m) -> p g m t", g=groups, t=PACK),
                 in_=in_.rearrange("p (g m t) -> p g m t", g=groups, t=PACK),
             )
 
-        rw_ps = psum_p.tile([P, 2, P], F32, name="rw_ps", tag="p_ps")
-        for e in range(2):
-            nc.tensor.transpose(rw_ps[:, e, :], rw_col[:, e : e + 1].to_broadcast([P, P]), ident[:])
-        rw_row = keep.tile([P, J], F32, name="rw_row")
-        nc.scalar.copy(out=rw_row[:].rearrange("p (n e) -> p n e", e=2), in_=rw_ps[:].rearrange("p e n -> p n e"))
-
         for i in range(PASSES * PACK):
             gather_b(i)
 
+        def turn_rows(rows, cols):
+            turned = psum_p.tile([P, PACK, P], F32, name="turned", tag="p_ps")
+            for t in range(PACK):
+                nc.tensor.transpose(turned[:, t, :], rows[:, t : P * PACK : PACK], ident[:])
+            nc.scalar.copy(out=cols[:], in_=turned[:, :, 0 : cols.shape[2]])
+
+        turn_rows(vec_rows, vec_cols)
+
         w_sc = keep.tile([P, PASSES * R], U8, name="w_sc", align_bytes=64)
-        deal(w_sc[:], w_sc_raw[:], PASSES)
-        wb_sc = keep.tile([P, N], U8, name="wb_sc", align_bytes=64)
-        deal(wb_sc[:], wb_sc_raw[:], 1)
+        deal_narrow(w_sc[:], w_sc_raw[:], PASSES)
         wb_dealt = keep.tile([P, N], U16, name="wb_dealt", align_bytes=64)
-        deal(wb_dealt[:], wb_raw[:].bitcast(U16), 1)
+        deal_narrow(wb_dealt[:], wb_raw[:].bitcast(U16), 1)
+        wb_sc = keep.tile([P, N], U8, name="wb_sc", align_bytes=64)
+        deal_narrow(wb_sc[:], wb_sc_raw[:], 1)
         for i in range(PACK):
             whole_plane(i)
-        neg_hi = keep.tile([P, PACK], F32, name="neg_hi")
-        nc.scalar.activation(neg_hi[:], hi_sb[:], ACT.Copy, scale=-1.0)
         quantize(u_codes[0], u_scales[0], u_bf[0], slice(0, J), E5M2X4)
+
+        late_cols = keep.tile([P, PACK, LATE_ROWS], F32, name="late_cols")
+        turn_rows(late_rows, late_cols)
+        neg_hi = keep.tile([P, PACK], F32, name="neg_hi")
+        nc.scalar.activation(neg_hi[:], late_cols[:, :, ROW_HI], ACT.Copy, scale=-1.0)
+        rw_ps = psum_p.tile([P, PACK, P], F32, name="rw_ps", tag="p_ps")
+        for t in range(PACK):
+            nc.tensor.transpose(rw_ps[:, t, :], late_cols[:, t, ROW_RW : ROW_RW + 1].to_broadcast([P, P]), ident[:])
+        rw_row = keep.tile([P, J], F32, name="rw_row")
+        nc.scalar.copy(
+            out=rw_row[:].rearrange("p (n t) -> p n t", t=PACK),
+            in_=rw_ps[:, :, 0 : J // PACK].rearrange("p t n -> p n t"),
+        )
+
         whole_plane(4)
         whole_plane(5)
         w_dealt = [keep.tile([P, R], I32, name=f"w_dealt{a}", align_bytes=64) for a in range(PASSES)]
@@ -182,11 +206,11 @@ def tile_list_boundedgaps_abovetable_capped_pl_kernel(
         last = PASSES * PACK - 1
         ga = ring.tile([P, J], F32, name="ga")
         neg_gap = ring.tile([P, J], F32, name="neg_gap")
-        nc.scalar.activation(ga[:, half_cols(0)], xa_planes[last].indirect(half_list(list_a, 0)), ACT.Copy)
-        nc.vector.tensor_copy(ga[:, half_cols(1)], xa_planes[last].indirect(half_list(list_a, 1)))
         for h in range(2):
-            gap(last, ga, neg_gap, half_cols(h))
+            nc.scalar.activation(ga[:, half_cols(h)], xa_planes[last].indirect(half_list(list_a, h)), ACT.Copy)
+        gap(last, ga, neg_gap, half_cols(0))
         deal(w_dealt[1][:], w_raw[1][:], 1)
+        gap(last, ga, neg_gap, half_cols(1))
         for h in range(2):
             scale_u(last, neg_gap, half_cols(h))
         for h in range(2):
@@ -253,7 +277,7 @@ def tile_list_boundedgaps_abovetable_capped_pl_kernel(
                 )
                 if h == 0 and t % 2 == 0:
                     nc.vector.tensor_scalar(
-                        out=below[h][:, t, :], in0=p_ps[:], scalar1=hi_sb[:, t : t + 1], scalar2=None, op0=ALU.subtract
+                        out=below[h][:, t, :], in0=p_ps[:], scalar1=late_cols[:, t, ROW_HI : ROW_HI + 1], scalar2=None, op0=ALU.subtract
                     )
                 else:
                     nc.scalar.activation(below[h][:, t, :], p_ps[:], ACT.Identity, bias=neg_hi[:, t : t + 1])
@@ -275,9 +299,10 @@ def tile_list_boundedgaps_abovetable_capped_pl_kernel(
         nc.vector.tensor_copy(out=woven(y_bf[:, HALF + quarter : J, :]), in_=by_plane(y[1][:, :, quarter:HALF]))
         for h in range(2):
             quantize(y_codes, y_scales, y_bf, half_cols(h), E4M3X4)
-            nc.sync.dma_start(out=words_out[:, half_cols(h)], in_=y_codes[:, half_cols(h)].bitcast(I32))
+            queue = nc.sync if h == 0 else nc.scalar
+            queue.dma_start(out=words_out[:, half_cols(h)], in_=y_codes[:, half_cols(h)].bitcast(I32))
         for q in range(4):
-            queue = nc.scalar if q < 2 else nc.sync
+            queue = nc.scalar if q == 3 else nc.sync
             queue.dma_start(
                 out=out_2[0, 4 * q : 4 * q + 4, :].bitcast(I32), in_=y_scales[32 * q : 32 * q + 4, :].bitcast(I32)
             )

from contextlib import ExitStack

import concourse.mybir as mybir
from concourse.masks import make_identity

K, T, J, S, R, V, N = 1024, 1024, 256, 512, 512, 512, 512
FLOPS = 2 * K * R * J + 2 * R * N * J

F32 = mybir.dt.float32
BF16 = mybir.dt.bfloat16
I32 = mybir.dt.int32
U32 = mybir.dt.uint32
U16 = mybir.dt.uint16
U8 = mybir.dt.uint8
E5M2X4 = mybir.dt.float8_e5m2_x4
E4M3X4 = mybir.dt.float8_e4m3fn_x4
E2M1X4 = mybir.dt.float4_e2m1fn_x4
ALU = mybir.AluOpType
ACT = mybir.ActivationFunctionType

P = 128
PACK = 4
PASSES = K // (P * PACK)
HALF = J // 2
LIST_COLS = J // 16
ROW_HB, ROW_FK, VEC_ROWS = 0, 2, 4
ROW_HI, ROW_RW, LATE_ROWS = 0, 1, 2


def tile_list_boundedgaps_abovetable_capped_pl_kernel(
    tc, xa, xb, hb, fk, w_words, w_scales, tb, wb_words, wb_scales, hi, rw, offs, offs2, offs3, out_0, out_1, out_2
):
    nc = tc.nc
    with ExitStack() as ctx:
        keep = ctx.enter_context(tc.tile_pool(name="keep", bufs=1))
        ring = ctx.enter_context(tc.tile_pool(name="ring", bufs=3))
        psum = ctx.enter_context(tc.psum_pool(name="psum", bufs=1))
        psum_p = ctx.enter_context(tc.psum_pool(name="psum_p", bufs=6))

        def half_cols(h):
            return slice(h * HALF, (h + 1) * HALF)

        def half_list(list_tile, h):
            return list_tile[:, h * LIST_COLS // 2 : (h + 1) * LIST_COLS // 2]

        w_sc_raw = keep.tile([P, PASSES * R], U8, name="w_sc_raw")
        wb_sc_raw = keep.tile([P, N], U8, name="wb_sc_raw")
        ident = keep.tile([P, P], F32, name="ident")
        nc.gpsimd.memset(w_sc_raw[:].bitcast(I32), 0)
        nc.gpsimd.memset(wb_sc_raw[:].bitcast(I32), 0)

        def load_scale_rows(queue, tile, scales, q):
            queue.dma_start(
                out=tile[32 * q : 32 * q + 4, :].bitcast(I32).rearrange("r (a c) -> r a c", a=scales.shape[0]),
                in_=scales[:, 4 * q : 4 * q + 4, :].bitcast(I32).rearrange("a r c -> r a c"),
            )

        for q in range(4):
            load_scale_rows(nc.gpsimd, wb_sc_raw, wb_scales, q)
        make_identity(nc, ident[:])

        vec_rows = keep.tile([P, P * PACK], F32, name="vec_rows")
        nc.vector.memset(vec_rows[:], 0.0)
        late_rows = keep.tile([P, P * PACK], F32, name="late_rows")
        nc.vector.memset(late_rows[:], 0.0)

        def load_vec(tile, row, src):
            nc.sync.dma_start(out=tile[row : row + src.shape[0], 0 : src.shape[1]], in_=src)

        xa_rows = xa.rearrange("(a p t) c -> a p t c", p=P, t=PACK)
        xb_rows = xb.rearrange("(a p t) c -> a p t c", p=P, t=PACK)
        tb_rows = tb.rearrange("(p t) c -> p t c", t=PACK)

        def load_list(name, src):
            tile = keep.tile([P, LIST_COLS], U16, name=name)
            nc.sync.dma_start(tile[:], src)
            return tile

        def load_rows(name, rows, t0, count):
            tile = keep.tile([P, count, rows.shape[2]], F32, name=name)
            nc.sync.dma_start(out=tile[:], in_=rows[:, t0 : t0 + count, :])
            return [tile[:, i, :] for i in range(count)]

        def load_words(name, src):
            tile = keep.tile([P, src.shape[1]], I32, name=name)
            nc.sync.dma_start(out=tile[:], in_=src)
            return tile

        def load_w(a):
            return load_words(f"w_raw{a}", w_words[a].rearrange("p c t -> p (c t)").bitcast(I32))

        list_b = load_list("list_b", offs2)
        xb_planes = load_rows("xb_0", xb_rows[0], 0, 4)
        for q in range(4):
            load_scale_rows(nc.sync, w_sc_raw, w_scales, q)
        xb_planes = xb_planes + load_rows("xb_1", xb_rows[1], 0, 4)
        load_vec(vec_rows, ROW_HB, hb.rearrange("(a c) o -> a (c o)", a=PASSES))
        load_vec(vec_rows, ROW_FK, fk.rearrange("(a c) o -> a (c o)", a=PASSES))
        wb_raw = load_words("wb_raw", wb_words[0].bitcast(I32))
        list_a = load_list("list_a", offs)
        xa_planes = [load_rows(f"xa_{t}", xa_rows[0], t, 1)[0] for t in range(PACK)]
        load_vec(late_rows, ROW_RW, rw)
        load_vec(late_rows, ROW_HI, hi.rearrange("(a c) o -> a (c o)", a=1))
        xa_planes = xa_planes + load_rows("xa_4", xa_rows[1], 0, 1)
        xa_planes = xa_planes + load_rows("xa_5", xa_rows[1], 1, 1)
        list_t = load_list("list_t", offs3)
        xa_planes = xa_planes + load_rows("xa_6", xa_rows[1], 2, 1)
        w_raw = [load_w(0)]
        xa_planes = xa_planes + load_rows("xa_7", xa_rows[1], 3, 1)
        w_raw = w_raw + [load_w(1)]
        tb_planes = [load_rows(f"tb_{t}", tb_rows, t, 1)[0] for t in range(PACK)]

        vec_cols = keep.tile([P, PACK, VEC_ROWS], F32, name="vec_cols")

        def vec_col(row, t):
            return vec_cols[:, t, row : row + 1]

        gb = [keep.tile([P, J], F32, name=f"gb{i}") for i in range(PASSES * PACK)]
        u_bf = [keep.tile([P, J, PACK], BF16, name=f"u_bf{a}", align_bytes=64) for a in range(PASSES)]
        u_codes = [keep.tile([P, J], U32, name=f"u_codes{a}", align_bytes=64) for a in range(PASSES)]
        u_scales = [keep.tile([P, J], U8, name=f"u_scales{a}", align_bytes=64) for a in range(PASSES)]

        def gather_b(i):
            if i % PACK < 2:
                nc.vector.tensor_copy(gb[i][:], xb_planes[i].indirect(list_b[:]))
            else:
                nc.scalar.activation(gb[i][:], xb_planes[i].indirect(list_b[:]), ACT.Copy)

        def gap(i, ga, neg_gap, cols):
            nc.vector.scalar_tensor_tensor(
                out=neg_gap[:, cols], in0=gb[i][:, cols], scalar=vec_col(ROW_HB + i // PACK, i % PACK), in1=ga[:, cols],
                op0=ALU.min, op1=ALU.subtract,
            )

        def scale_u(i, neg_gap, cols):
            nc.vector.tensor_scalar(
                out=u_bf[i // PACK][:, cols, i % PACK], in0=neg_gap[:, cols], scalar1=vec_col(ROW_FK + i // PACK, i % PACK),
                scalar2=-1.0, op0=ALU.mult, op1=ALU.mult,
            )

        def quantize(codes, scales, values, cols, x4):
            nc.vector.quantize_mx(
                out=codes[:, cols].bitcast(x4), scales=scales[:, cols],
                in_=values[:, cols, :].rearrange("p j t -> p (j t)"),
            )

        def whole_plane(i):
            ga = ring.tile([P, J], F32, name="ga")
            neg_gap = ring.tile([P, J], F32, name="neg_gap")
            nc.scalar.activation(ga[:], xa_planes[i].indirect(list_a[:]), ACT.Copy)
            gap(i, ga, neg_gap, slice(0, J))
            scale_u(i, neg_gap, slice(0, J))

        def deal_narrow(out, in_, groups):
            nc.vector.tensor_copy(
                out=out.rearrange("p (g t m) -> p g t m", g=groups, t=PACK),
                in_=in_.rearrange("p (g m t) -> p g t m", g=groups, t=PACK),
            )

        def deal(out, in_, groups):
            nc.vector.tensor_copy(
                out=out.rearrange("p (g t m) -> p g m t", g=groups, t=PACK),
                in_=in_.rearrange("p (g m t) -> p g m t", g=groups, t=PACK),
            )

        for i in range(PASSES * PACK):
            gather_b(i)

        def turn_rows(rows, cols):
            turned = psum_p.tile([P, PACK, P], F32, name="turned", tag="p_ps")
            for t in range(PACK):
                nc.tensor.transpose(turned[:, t, :], rows[:, t : P * PACK : PACK], ident[:])
            nc.scalar.copy(out=cols[:], in_=turned[:, :, 0 : cols.shape[2]])

        turn_rows(vec_rows, vec_cols)

        w_sc = keep.tile([P, PASSES * R], U8, name="w_sc", align_bytes=64)
        deal_narrow(w_sc[:], w_sc_raw[:], PASSES)
        wb_dealt = keep.tile([P, N], U16, name="wb_dealt", align_bytes=64)
        deal_narrow(wb_dealt[:], wb_raw[:].bitcast(U16), 1)
        wb_sc = keep.tile([P, N], U8, name="wb_sc", align_bytes=64)
        deal_narrow(wb_sc[:], wb_sc_raw[:], 1)
        for i in range(PACK):
            whole_plane(i)
        quantize(u_codes[0], u_scales[0], u_bf[0], slice(0, J), E5M2X4)

        late_cols = keep.tile([P, PACK, LATE_ROWS], F32, name="late_cols")
        turn_rows(late_rows, late_cols)
        neg_hi = keep.tile([P, PACK], F32, name="neg_hi")
        nc.scalar.activation(neg_hi[:], late_cols[:, :, ROW_HI], ACT.Copy, scale=-1.0)
        rw_ps = psum_p.tile([P, PACK, P], F32, name="rw_ps", tag="p_ps")
        for t in range(PACK):
            nc.tensor.transpose(rw_ps[:, t, :], late_cols[:, t, ROW_RW : ROW_RW + 1].to_broadcast([P, P]), ident[:])
        rw_row = keep.tile([P, J], F32, name="rw_row")
        nc.scalar.copy(
            out=rw_row[:].rearrange("p (n t) -> p n t", t=PACK),
            in_=rw_ps[:, :, 0 : J // PACK].rearrange("p t n -> p n t"),
        )

        whole_plane(4)
        whole_plane(5)
        w_dealt = [keep.tile([P, R], I32, name=f"w_dealt{a}", align_bytes=64) for a in range(PASSES)]
        deal(w_dealt[0][:], w_raw[0][:], 1)
        whole_plane(6)

        last = PASSES * PACK - 1
        ga = ring.tile([P, J], F32, name="ga")
        neg_gap = ring.tile([P, J], F32, name="neg_gap")
        for h in range(2):
            nc.scalar.activation(ga[:, half_cols(h)], xa_planes[last].indirect(half_list(list_a, h)), ACT.Copy)
        gap(last, ga, neg_gap, half_cols(0))
        deal(w_dealt[1][:], w_raw[1][:], 1)
        gap(last, ga, neg_gap, half_cols(1))
        for h in range(2):
            scale_u(last, neg_gap, half_cols(h))
        for h in range(2):
            quantize(u_codes[1], u_scales[1], u_bf[1], half_cols(h), E5M2X4)

        a_ps = [psum.tile([P, PACK, HALF], F32, name=f"a_ps{h}", tag=f"a_ps{h}") for h in range(2)]
        for a in range(PASSES):
            for h in range(2):
                for t in range(PACK):
                    nc.tensor.matmul_mx(
                        out=a_ps[h][:, t, :],
                        lhsT=w_dealt[a][:, t * P : (t + 1) * P].bitcast(E5M2X4),
                        lhsT_scale=w_sc[:, a * R + t * P : a * R + (t + 1) * P],
                        rhs=u_codes[a][:, half_cols(h)].bitcast(E5M2X4),
                        rhs_scale=u_scales[a][:, half_cols(h)],
                        start=(a == 0 and t == 0),
                        stop=(a == PASSES - 1 and t == PACK - 1),
                    )

        gt = keep.tile([P, PACK, J], F32, name="gt")
        for t in range(2):
            nc.scalar.activation(gt[:, t, :], tb_planes[t].indirect(list_t[:]), ACT.Copy)
        for t, h in ((2, 0), (3, 0), (2, 1)):
            nc.scalar.activation(gt[:, t, half_cols(h)], tb_planes[t].indirect(half_list(list_t, h)), ACT.Copy)
        nc.vector.tensor_copy(gt[:, 3, half_cols(1)], tb_planes[3].indirect(half_list(list_t, 1)))

        def woven(values):
            return values.rearrange("p (c i) t -> p c t i", i=4)

        def by_plane(values):
            return values.rearrange("p t (c i) -> p c t i", i=4)

        hid_bf = keep.tile([P, J, PACK], BF16, name="hid_bf", align_bytes=64)
        hid_codes = keep.tile([P, J], U32, name="hid_codes", align_bytes=64)
        hid_scales = keep.tile([P, J], U8, name="hid_scales", align_bytes=64)
        for h in range(2):
            nc.vector.tensor_tensor(
                out=woven(hid_bf[:, half_cols(h), :]), in0=by_plane(a_ps[h][:]),
                in1=by_plane(gt[:, :, half_cols(h)]), op=ALU.max,
            )
            quantize(hid_codes, hid_scales, hid_bf, half_cols(h), E5M2X4)

        y_rows = out_0.rearrange("(p t) j -> p t j", t=PACK)
        y_bf = keep.tile([P, J, PACK], BF16, name="y_bf", align_bytes=64)
        y_codes = keep.tile([P, J], U32, name="y_codes", align_bytes=64)
        y_scales = keep.tile([P, J], U8, name="y_scales", align_bytes=64)
        words_out = out_1[0].rearrange("p j t -> p (j t)").bitcast(I32)
        below = [keep.tile([P, PACK, HALF], F32, name=f"below{h}") for h in range(2)]
        y = [keep.tile([P, PACK, HALF], F32, name=f"y{h}") for h in range(2)]
        for h in range(2):
            for t in range(PACK):
                if h == 1 and t >= 2:
                    p_ps = psum.tile([P, HALF], F32, name="p_ps", tag=f"a_ps{t - 2}")
                else:
                    p_ps = psum_p.tile([P, HALF], F32, name="p_ps", tag="p_ps")
                nc.tensor.matmul_mx(
                    out=p_ps[:],
                    lhsT=wb_dealt[:, t * P : (t + 1) * P].bitcast(E2M1X4),
                    lhsT_scale=wb_sc[:, t * P : (t + 1) * P],
                    rhs=hid_codes[:, half_cols(h)].bitcast(E5M2X4),
                    rhs_scale=hid_scales[:, half_cols(h)],
                    start=True,
                    stop=True,
                )
                if h == 0 and t % 2 == 0:
                    nc.vector.tensor_scalar(
                        out=below[h][:, t, :], in0=p_ps[:], scalar1=late_cols[:, t, ROW_HI : ROW_HI + 1], scalar2=None, op0=ALU.subtract
                    )
                else:
                    nc.scalar.activation(below[h][:, t, :], p_ps[:], ACT.Identity, bias=neg_hi[:, t : t + 1])
        def weigh(h, c0, c1):
            nc.vector.scalar_tensor_tensor(
                out=y[h][:, :, c0:c1], in0=below[h][:, :, c0:c1], scalar=0.0,
                in1=rw_row[:, h * HALF + c0 : h * HALF + c1].unsqueeze(1).to_broadcast([P, PACK, c1 - c0]),
                op0=ALU.min, op1=ALU.mult,
            )

        quarter = HALF // 2
        weigh(0, 0, HALF)
        nc.sync.dma_start(out=y_rows[:, :, half_cols(0)], in_=y[0][:])
        nc.scalar.copy(out=woven(y_bf[:, half_cols(0), :]), in_=by_plane(y[0][:]))
        weigh(1, 0, quarter)
        weigh(1, quarter, HALF)
        nc.sync.dma_start(out=y_rows[:, :, half_cols(1)], in_=y[1][:])
        nc.vector.tensor_copy(out=woven(y_bf[:, HALF : HALF + quarter, :]), in_=by_plane(y[1][:, :, 0:quarter]))
        nc.vector.tensor_copy(out=woven(y_bf[:, HALF + quarter : J, :]), in_=by_plane(y[1][:, :, quarter:HALF]))
        for h in range(2):
            quantize(y_codes, y_scales, y_bf, half_cols(h), E4M3X4)
            queue = nc.sync if h == 0 else nc.scalar
            queue.dma_start(out=words_out[:, half_cols(h)], in_=y_codes[:, half_cols(h)].bitcast(I32))
        for q in range(4):
            queue = nc.scalar if q == 3 else nc.sync
            queue.dma_start(
                out=out_2[0, 4 * q : 4 * q + 4, :].bitcast(I32), in_=y_scales[32 * q : 32 * q + 4, :].bitcast(I32)
            )
